import numpy as np
import ml_dtypes


def mxq(x, axis, fmt="e4m3"):
    dtype, down = {"e4m3": (ml_dtypes.float8_e4m3fn, 7), "e5m2": (ml_dtypes.float8_e5m2, 14)}[fmt]
    v = np.moveaxis(np.asarray(x, np.float32).astype(ml_dtypes.bfloat16).astype(np.float64), axis, -1)
    blocks = v.reshape(v.shape[:-1] + (-1, 32))
    amax = np.abs(blocks).max(-1, keepdims=True)
    byte = np.maximum(np.where(amax > 0, np.frexp(amax)[1] - 1 + 127, 0) - down, 1)
    scale = np.exp2(byte - 127.0)
    codes = (blocks / scale).astype(np.float32).astype(dtype).astype(np.float64)
    return np.moveaxis((codes * scale).reshape(v.shape), -1, axis)


WIDE = False


def mx_kscale(k):
    if not WIDE:
        return np.ones(k)
    levels = np.array([10, -10, 5, -5, 0])
    if k % 512:
        return np.exp2(np.random.permutation(np.resize(levels, k // 32))).repeat(32)
    a = np.empty((k // 512, 16))
    for p in range(k // 512):
        a[p, :8] = np.random.permutation(np.resize(levels, 8))
        for g in range(8):
            far = levels[np.abs(levels - a[p, g]) >= 10]
            a[p, g + 8] = far[np.random.randint(len(far))]
    return np.exp2(a.ravel()).repeat(32)


def f64(x):
    return np.asarray(x).astype(np.float64)


def striped(idx):
    return np.tile(idx.reshape(-1, 16).T, (8, 1)).astype(np.uint16)


def unstriped(offs):
    return offs[:16].T.reshape(-1).astype(np.int64)


def striped8(idx):
    return np.concatenate([x.reshape(-1, 16).T for x in idx]).astype(np.uint16)


def runs(offs, k):
    lists = np.stack([offs[16 * r : 16 * r + 16].T.reshape(-1) for r in range(8)]).astype(np.int64)
    return lists[np.arange(k) % 512 // 64]


def pack_weight(w):
    k, n = w.shape
    w = f64(np.asarray(w, np.float32).astype(ml_dtypes.bfloat16)).reshape(k // 32, 32, n)
    amax = np.abs(w).max(1)
    byte = np.clip(np.where(amax > 0, np.frexp(amax)[1] - 1 + 127 - 7, 1), 1, 254)
    scaled = (w * np.exp2(127.0 - byte)[:, None, :]).reshape(k, n).astype(np.float32)
    words = np.ascontiguousarray(scaled.reshape(k // 512, 128, 4, n).transpose(0, 1, 3, 2)).astype(ml_dtypes.float8_e4m3fn).view(np.uint8)
    return words, np.ascontiguousarray(byte.astype(np.uint8).reshape(k // 512, 16, n))


def unpack_weight(words, scales):
    g, p, n, _ = words.shape
    vals = np.ascontiguousarray(words).view(ml_dtypes.float8_e4m3fn).astype(np.float64) * np.repeat(np.exp2(scales.astype(np.float64) - 127.0), 8, axis=1)[..., None]
    return vals.transpose(0, 1, 3, 2).reshape(g * 512, n)


E2M1 = np.array([0.0, 0.5, 1.0, 1.5, 2.0, 3.0, 4.0, 6.0, -0.0, -0.5, -1.0, -1.5, -2.0, -3.0, -4.0, -6.0])


def pack_fp4(w):
    k, n = w.shape
    w = f64(np.asarray(w, np.float32).astype(ml_dtypes.bfloat16)).reshape(k // 32, 32, n)
    amax = np.abs(w).max(1)
    mant, ex = np.frexp(amax / 6.0)
    byte = np.clip(np.where(amax > 0, np.where(mant > 0.5, ex, ex - 1) + 127, 1), 1, 254)
    scaled = (w * np.exp2(127.0 - byte)[:, None, :]).reshape(k, n).astype(np.float32)
    c = np.ascontiguousarray(scaled.reshape(k // 512, 128, 4, n).transpose(0, 1, 3, 2)).astype(ml_dtypes.float4_e2m1fn).view(np.uint8) & 0xF
    words = (c[..., 0::2] | (c[..., 1::2] << 4)).reshape(k // 512, 128, 2 * n)
    return np.ascontiguousarray(words), np.ascontiguousarray(byte.astype(np.uint8).reshape(k // 512, 16, n))


def unpack_fp4(words, scales):
    g, _, n = scales.shape
    words = np.ascontiguousarray(words).reshape(g, 128, n, 2)
    nib = np.empty((g, 128, n, 4), np.uint8)
    nib[..., 0::2] = words & 0xF
    nib[..., 1::2] = words >> 4
    vals = E2M1[nib] * np.repeat(np.exp2(scales.astype(np.float64) - 127.0), 8, axis=1)[..., None]
    return vals.transpose(0, 1, 3, 2).reshape(g * 512, n)


K, T, S, H, W, G = 512, 1024, 512, 512, 256, 2048


def setup_inputs():
    n = np.random.standard_normal
    s = mx_kscale(K)[:, None]
    packed_xT = pack_weight(n((K, T)) * s)
    packed_w1 = pack_fp4(n((K, H)) / np.sqrt(K) / s)
    packed_dT = pack_weight(n((K, G)) / s)
    perm = np.random.permutation(S)
    perm2 = np.stack([np.random.permutation(S) for _ in range(8)])
    return {
        "x_words": packed_xT[0],
        "x_scales": packed_xT[1],
        "w1_words": packed_w1[0],
        "w1_scales": packed_w1[1],
        "gs": (np.random.uniform(0.5, 1.5, (K, 1)) * s).astype(np.float32),
        "d_words": packed_dT[0],
        "d_scales": packed_dT[1],
        "offs": striped(np.random.permutation(T)[:S]),
        "n1": striped(perm[:W]),
        "n2": striped(perm[W:]),
        "n3": striped(np.random.permutation(S)),
        "k1": striped8(np.random.randint(0, G, (8, H))),
        "k2": striped8(np.random.randint(0, G, (8, H))),
        "hz": striped8(np.random.randint(0, T, (8, S))),
        "n4": striped8(perm2[:, :W]),
        "n5": striped8(perm2[:, W:]),
    }


def reference(x_words, x_scales, w1_words, w1_scales, gs, d_words, d_scales, offs, n1, n2, n3, k1, k2, hz, n4, n5):
    d_k1 = unpack_weight(d_words, d_scales)[np.arange(K)[:, None], runs(k1, K)]
    xq = unpack_weight(x_words, x_scales)[:, unstriped(offs)]
    y = unpack_fp4(w1_words, w1_scales).T @ xq
    pa = y[:, unstriped(n1)]
    pb = y[:, unstriped(n2)]
    rb = pa - pb
    ra = pa + pb
    ds = np.zeros((H, S))
    ds[:, unstriped(n1)] = ra
    dt = ds.copy()
    dt[:, unstriped(n2)] = rb
    z = f64(gs) * (np.maximum(dt, dt[:, unstriped(n3)]))
    d_k2 = unpack_weight(d_words, d_scales)[np.arange(K)[:, None], runs(k2, K)]
    x_hz = unpack_weight(x_words, x_scales)[np.arange(K)[:, None], runs(hz, K)]
    h = 0.0625 * ((d_k1.T @ mxq(z, 0, "e4m3") + d_k2.T @ x_hz))
    pb2 = h[np.arange(H)[:, None], runs(n5, H)]
    pa2 = h[np.arange(H)[:, None], runs(n4, H)]
    rb2 = pb2 - (0.5 * pa2)
    ra2 = np.sqrt((pa2) ** 2 + (pb2) ** 2 + 0.25)
    ds2 = np.zeros((H, S))
    ds2[np.arange(H)[:, None], runs(n4, H)] = ra2
    out = ds2.copy()
    out[np.arange(H)[:, None], runs(n5, H)] = rb2
    return out

@@ -1,0 +1,236 @@
+from contextlib import ExitStack
+
+import concourse.mybir as mybir
+
+F32 = mybir.dt.float32
+BF16 = mybir.dt.bfloat16
+I32 = mybir.dt.int32
+U32 = mybir.dt.uint32
+U16 = mybir.dt.uint16
+U8 = mybir.dt.uint8
+FP8X4 = mybir.dt.float8_e4m3fn_x4
+FP4X4 = mybir.dt.float4_e2m1fn_x4
+ACT = mybir.ActivationFunctionType
+ALU = mybir.AluOpType
+
+P = 128
+PACK = 4
+K, T, S, H, W, G = 512, 1024, 512, 512, 256, 2048
+FLOPS = 3 * 2 * K * H * S
+
+
+def tile_picked_cmixhhaarhpolar_none_p_kernel(
+    tc, x_words, x_scales, w1_words, w1_scales, gs, d_words, d_scales, offs, n1, n2, n3, k1, k2, hz, n4, n5, out
+):
+    nc = tc.nc
+    with ExitStack() as ctx:
+        keep = ctx.enter_context(tc.tile_pool(name="keep", bufs=1))
+        psum = ctx.enter_context(tc.psum_pool(name="psum", bufs=1))
+
+        def sb(name, cols, dtype, tag=None):
+            return keep.tile([P, cols], dtype, name=name, tag=tag or name, align_bytes=64)
+
+        def load_list(name, src):
+            tile = keep.tile([P, src.shape[1]], U16, name=name)
+            nc.sync.dma_start(tile[:], src)
+            return tile
+
+        x_bytes = sb("x_bytes", T, U8)
+        d_bytes = sb("d_bytes", G, U8)
+        w_bytes = sb("w_bytes", H, U8)
+        placed = sb("placed", 3 * S, U8)
+        quarter = sb("quarter", 1, F32)
+        nc.gpsimd.memset(x_bytes[:].bitcast(I32), 0)
+        nc.gpsimd.memset(w_bytes[:].bitcast(I32), 0)
+        nc.gpsimd.memset(d_bytes[:].bitcast(I32), 0)
+        nc.gpsimd.dma_start(d_bytes[0:P:8, :].bitcast(I32), d_scales[0].bitcast(I32))
+        nc.vector.memset(placed[:].bitcast(I32), 0)
+        nc.vector.memset(quarter[:], 0.25)
+
+        x_tab = sb("x_tab", T, U32)
+        w_raw = sb("w_raw", 2 * H, U8)
+        gain = sb("gain", PACK, F32)
+
+        l_offs = load_list("l_offs", offs)
+        nc.sync.dma_start(x_bytes[0:P:8, :].bitcast(I32), x_scales[0].bitcast(I32))
+        for r in range(1, PACK):
+            nc.sync.dma_start(x_bytes[r:P:32, :].bitcast(I32), x_scales[0][r:16:PACK, :].bitcast(I32))
+        nc.sync.dma_start(x_tab[:].bitcast(I32), x_words[0].rearrange("p n t -> p (n t)").bitcast(I32))
+        nc.sync.dma_start(w_raw[:].bitcast(I32), w1_words[0].bitcast(I32))
+        l_hz = load_list("l_hz", hz)
+        for r in range(PACK):
+            nc.sync.dma_start(w_bytes[r:P:32, :].bitcast(I32), w1_scales[0][r:16:PACK, :].bitcast(I32))
+        l_k1 = load_list("l_k1", k1)
+        l_k2 = load_list("l_k2", k2)
+        l_n1 = load_list("l_n1", n1)
+        l_n2 = load_list("l_n2", n2)
+        l_n3 = load_list("l_n3", n3)
+        nc.gpsimd.dma_start(gain[:], gs.rearrange("(p t) o -> p (t o)", t=PACK))
+        l_n4 = load_list("l_n4", n4)
+        l_n5 = load_list("l_n5", n5)
+
+        xq_scale = sb("xq_scale", S, U8)
+        xq_word = sb("xq_word", S, U32)
+        nc.vector.tensor_copy(xq_scale[:], x_bytes[:].indirect(l_offs[:]))
+        nc.vector.tensor_copy(xq_word[:], x_tab[:].indirect(l_offs[:]))
+        w_word = sb("w_word", 2 * H, U8)
+        w_scale = sb("w_scale", H, U8)
+        nc.scalar.copy(
+            w_word[:].bitcast(U16).rearrange("p (t m) -> p t m", t=PACK),
+            w_raw[:].bitcast(U16).rearrange("p (m t) -> p t m", t=PACK),
+        )
+        nc.vector.tensor_copy(
+            w_scale[:].rearrange("p (t m) -> p m t", t=PACK), w_bytes[:].rearrange("p (m t) -> p m t", t=PACK)
+        )
+        d_tab = sb("d_tab", G, U32, tag="w_raw")
+        nc.sync.dma_start(d_tab[:].bitcast(I32), d_words[0].rearrange("p n t -> p (n t)").bitcast(I32))
+        y_bank = [psum.tile([P, S], F32, name=f"y_bank{t}") for t in range(PACK)]
+        for t in range(PACK):
+            nc.tensor.matmul_mx(
+                out=y_bank[t][:],
+                lhsT=w_word[:, 2 * P * t : 2 * P * (t + 1)].bitcast(FP4X4),
+                lhsT_scale=w_scale[:, P * t : P * (t + 1)],
+                rhs=xq_word[:].bitcast(FP8X4),
+                rhs_scale=xq_scale[:],
+                start=True,
+                stop=True,
+            )
+
+        picked = sb("picked", 3 * S, U8)
+        nc.vector.tensor_copy(picked[:, 2 * S : 3 * S], x_bytes[:].indirect(l_hz[:]))
+        xh_word = sb("xh_word", S, U32, tag="w_bytes")
+        nc.vector.tensor_copy(xh_word[:], x_tab[:].indirect(l_hz[:]))
+        nc.vector.tensor_copy(picked[:, 0:S], d_bytes[:].indirect(l_k1[:]))
+        nc.vector.tensor_copy(picked[:, S : 2 * S], d_bytes[:].indirect(l_k2[:]))
+        for r in range(PACK):
+            nc.sync.dma_start(placed[r:P:32, :].bitcast(I32), picked[8 * r : P : 32, :].bitcast(I32))
+
+        z_rows = keep.tile([P, S, PACK], BF16, name="z_rows", align_bytes=64)
+        dt = [sb(f"dt{t}", S, F32) for t in range(PACK)]
+
+        def pair_up(t):
+            y = sb(f"y{t}", S, F32)
+            pa = sb(f"pa{t}", W, F32)
+            pb = sb(f"pb{t}", W, F32)
+            pb_neg = sb(f"pb_neg{t}", W, F32)
+            nc.scalar.copy(y[:], y_bank[t][:])
+            nc.scalar.activation(pa[:], y[:].indirect(l_n1[:]), ACT.Copy)
+            nc.scalar.activation(pb[:], y[:].indirect(l_n2[:]), ACT.Copy)
+            nc.scalar.activation(pb_neg[:], pb[:], ACT.Copy, scale=-1.0)
+            nc.vector.tensor_tensor(dt[t][:].indirect(l_n1[:]), pa[:], pb[:], ALU.add)
+            nc.vector.tensor_tensor(dt[t][:].indirect(l_n2[:]), pa[:], pb_neg[:], ALU.add)
+
+        other = {}
+        top = {}
+
+        def fetch(t):
+            other[t] = sb(f"other{t}", S, F32)
+            for half in range(2):
+                nc.scalar.activation(
+                    other[t][:, W * half : W * (half + 1)],
+                    dt[t][:].indirect(l_n3[:, 16 * half : 16 * (half + 1)]),
+                    ACT.Copy,
+                )
+            top[t] = sb(f"top{t}", S, F32)
+            nc.vector.tensor_tensor(top[t][:], dt[t][:], other[t][:], ALU.max)
+
+        def weigh(t):
+            nc.scalar.activation(z_rows[:, :, t], top[t][:], ACT.Copy, scale=gain[:, t : t + 1])
+
+        def codewords(name, lst, tag):
+            got = sb(f"{name}_got", H, U32, tag=tag)
+            dealt = sb(f"{name}_word", H, U32)
+            nc.vector.tensor_copy(got[:], d_tab[:].indirect(lst[:]))
+            nc.vector.tensor_copy(
+                dealt[:].rearrange("p (t m) -> p m t", t=PACK), got[:].rearrange("p (m t) -> p m t", t=PACK)
+            )
+            return dealt
+
+        pair_up(0)
+        pair_up(1)
+        fetch(0)
+        pair_up(2)
+        fetch(1)
+        d_scale = sb("d_scale", 2 * S, U8, tag="pa1")
+        nc.vector.tensor_copy(
+            d_scale[:].rearrange("p (c t m) -> p c m t", c=2, t=PACK),
+            placed[:, 0 : 2 * S].rearrange("p (c m t) -> p c m t", c=2, t=PACK),
+        )
+        pair_up(3)
+        weigh(0)
+        fetch(2)
+        weigh(1)
+        d2_word = codewords("d2", l_k2, "pa3")
+        fetch(3)
+        weigh(2)
+        d1_word = codewords("d1", l_k1, "other3")
+        weigh(3)
+
+        z_word = sb("z_word", S, U32)
+        z_scale = sb("z_scale", S, U8)
+        nc.vector.quantize_mx(out=z_word[:].bitcast(FP8X4), scales=z_scale[:], in_=z_rows[:].rearrange("p c t -> p (c t)"))
+
+        h_bank = [psum.tile([P, S], F32, name=f"h_bank{t}") for t in range(PACK)]
+        for t in range(PACK):
+            nc.tensor.matmul_mx(
+                out=h_bank[t][:],
+                lhsT=d2_word[:, P * t : P * (t + 1)].bitcast(FP8X4),
+                lhsT_scale=d_scale[:, S + P * t : S + P * (t + 1)],
+                rhs=xh_word[:].bitcast(FP8X4),
+                rhs_scale=placed[:, 2 * S : 3 * S],
+                start=True,
+                stop=False,
+            )
+        for t in range(PACK):
+            nc.tensor.matmul_mx(
+                out=h_bank[t][:],
+                lhsT=d1_word[:, P * t : P * (t + 1)].bitcast(FP8X4),
+                lhsT_scale=d_scale[:, P * t : P * (t + 1)],
+                rhs=z_word[:].bitcast(FP8X4),
+                rhs_scale=z_scale[:],
+                start=False,
+                stop=True,
+            )
+
+        out_rows = out.rearrange("(p t) n -> t p n", t=PACK)
+        h = [sb(f"h{t}", S, F32) for t in range(PACK)]
+        pair = [sb(f"pair{t}", 2 * W, F32) for t in range(PACK)]
+        total = [sb(f"total{t}", W, F32) for t in range(PACK)]
+        result = [sb(f"result{t}", S, F32) for t in range(PACK)]
+
+        def leave_bank(t):
+            if t == 1:
+                nc.vector.tensor_scalar_mul(h[t][:], h_bank[t][:], 0.0625)
+            else:
+                nc.scalar.activation(h[t][:], h_bank[t][:], ACT.Copy, scale=0.0625)
+
+        def pick(t):
+            nc.scalar.activation(pair[t][:, 0:W], h[t][:].indirect(l_n4[:]), ACT.Copy, scale=-0.5)
+            if t == 0:
+                nc.vector.tensor_copy(pair[t][:, W : 2 * W], h[t][:].indirect(l_n5[:]))
+            else:
+                nc.scalar.activation(pair[t][:, W : 2 * W], h[t][:].indirect(l_n5[:]), ACT.Copy)
+            nc.vector.tensor_tensor(result[t][:].indirect(l_n5[:]), pair[t][:, 0:W], pair[t][:, W : 2 * W], ALU.add)
+
+        def squares(t):
+            square = sb(f"square{t}", 2 * W, F32)
+            nc.scalar.activation(square[:], pair[t][:], ACT.Square)
+            nc.vector.scalar_tensor_tensor(total[t][:], square[:, 0:W], 4.0, square[:, W : 2 * W], ALU.mult, ALU.add)
+
+        def finish(t):
+            root = sb(f"root{t}", W, F32)
+            nc.scalar.activation(root[:], total[t][:], ACT.Sqrt, bias=quarter[:])
+            nc.vector.tensor_copy(result[t][:].indirect(l_n4[:]), root[:])
+            nc.sync.dma_start(out_rows[t], result[t][:])
+
+        leave_bank(0)
+        leave_bank(1)
+        pick(0)
+        squares(0)
+        for t in range(1, PACK):
+            if t > 1:
+                leave_bank(t)
+            pick(t)
+            finish(t - 1)
+            squares(t)
+        finish(PACK - 1)

@@ -65,7 +65,7 @@ def tile_picked_cmixhhaarhpolar_none_p_kernel(
         l_n1 = load_list("l_n1", n1)
         l_n2 = load_list("l_n2", n2)
         l_n3 = load_list("l_n3", n3)
-        nc.gpsimd.dma_start(gain[:], gs.rearrange("(p t) o -> p (t o)", t=PACK))
+        nc.sync.dma_start(gain[:], gs.rearrange("(p t) o -> p (t o)", t=PACK))
         l_n4 = load_list("l_n4", n4)
         l_n5 = load_list("l_n5", n5)
 
@@ -84,7 +84,7 @@ def tile_picked_cmixhhaarhpolar_none_p_kernel(
         )
         d_tab = sb("d_tab", G, U32, tag="w_raw")
         nc.sync.dma_start(d_tab[:].bitcast(I32), d_words[0].rearrange("p n t -> p (n t)").bitcast(I32))
-        y_bank = [psum.tile([P, S], F32, name=f"y_bank{t}") for t in range(PACK)]
+        y_bank = [psum.tile([P, S], F32, name=f"y_bank{t}", tag=f"y_bank{t}") for t in range(PACK)]
         for t in range(PACK):
             nc.tensor.matmul_mx(
                 out=y_bank[t][:],
@@ -98,8 +98,6 @@ def tile_picked_cmixhhaarhpolar_none_p_kernel(
 
         picked = sb("picked", 3 * S, U8)
         nc.vector.tensor_copy(picked[:, 2 * S : 3 * S], x_bytes[:].indirect(l_hz[:]))
-        xh_word = sb("xh_word", S, U32, tag="w_bytes")
-        nc.vector.tensor_copy(xh_word[:], x_tab[:].indirect(l_hz[:]))
         nc.vector.tensor_copy(picked[:, 0:S], d_bytes[:].indirect(l_k1[:]))
         nc.vector.tensor_copy(picked[:, S : 2 * S], d_bytes[:].indirect(l_k2[:]))
         for r in range(PACK):
@@ -108,17 +106,26 @@ def tile_picked_cmixhhaarhpolar_none_p_kernel(
         z_rows = keep.tile([P, S, PACK], BF16, name="z_rows", align_bytes=64)
         dt = [sb(f"dt{t}", S, F32) for t in range(PACK)]
 
-        def pair_up(t):
-            y = sb(f"y{t}", S, F32)
-            pa = sb(f"pa{t}", W, F32)
-            pb = sb(f"pb{t}", W, F32)
+        pa = {}
+        pb = {}
+
+        y = {}
+
+        def first_members(t):
+            y[t] = sb(f"y{t}", S, F32)
+            pa[t] = sb(f"pa{t}", W, F32)
+            nc.scalar.activation(y[t][:], y_bank[t][:], ACT.Copy)
+            nc.scalar.activation(pa[t][:], y[t][:].indirect(l_n1[:]), ACT.Copy)
+
+        def pair_sum(t):
+            pb[t] = sb(f"pb{t}", W, F32)
+            nc.scalar.activation(pb[t][:], y[t][:].indirect(l_n2[:]), ACT.Copy)
+            nc.vector.tensor_tensor(dt[t][:].indirect(l_n1[:]), pa[t][:], pb[t][:], ALU.add)
+
+        def pair_difference(t):
             pb_neg = sb(f"pb_neg{t}", W, F32)
-            nc.scalar.copy(y[:], y_bank[t][:])
-            nc.scalar.activation(pa[:], y[:].indirect(l_n1[:]), ACT.Copy)
-            nc.scalar.activation(pb[:], y[:].indirect(l_n2[:]), ACT.Copy)
-            nc.scalar.activation(pb_neg[:], pb[:], ACT.Copy, scale=-1.0)
-            nc.vector.tensor_tensor(dt[t][:].indirect(l_n1[:]), pa[:], pb[:], ALU.add)
-            nc.vector.tensor_tensor(dt[t][:].indirect(l_n2[:]), pa[:], pb_neg[:], ALU.add)
+            nc.scalar.activation(pb_neg[:], pb[t][:], ACT.Copy, scale=-1.0)
+            nc.vector.tensor_tensor(dt[t][:].indirect(l_n2[:]), pa[t][:], pb_neg[:], ALU.add)
 
         other = {}
         top = {}
@@ -146,48 +153,59 @@ def tile_picked_cmixhhaarhpolar_none_p_kernel(
             )
             return dealt
 
-        pair_up(0)
-        pair_up(1)
-        fetch(0)
-        pair_up(2)
-        fetch(1)
-        d_scale = sb("d_scale", 2 * S, U8, tag="pa1")
+        first_members(0)
+        pair_sum(0)
+        first_members(1)
+        pair_sum(1)
+        pair_difference(0)
+        first_members(2)
+        pair_sum(2)
+        d_scale = sb("d_scale", 2 * S, U8, tag="y2")
         nc.vector.tensor_copy(
             d_scale[:].rearrange("p (c t m) -> p c m t", c=2, t=PACK),
             placed[:, 0 : 2 * S].rearrange("p (c m t) -> p c m t", c=2, t=PACK),
         )
-        pair_up(3)
+        pair_difference(1)
+        first_members(3)
+        fetch(0)
+        pair_sum(3)
+        pair_difference(2)
+        fetch(1)
+        pair_difference(3)
         weigh(0)
+        d2_word = codewords("d2", l_k2, "top0")
         fetch(2)
         weigh(1)
-        d2_word = codewords("d2", l_k2, "pa3")
+        xh_word = sb("xh_word", S, U32, tag="top1")
+        nc.vector.tensor_copy(xh_word[:], x_tab[:].indirect(l_hz[:]))
         fetch(3)
         weigh(2)
-        d1_word = codewords("d1", l_k1, "other3")
+        d1_word = codewords("d1", l_k1, "top2")
         weigh(3)
 
         z_word = sb("z_word", S, U32)
         z_scale = sb("z_scale", S, U8)
         nc.vector.quantize_mx(out=z_word[:].bitcast(FP8X4), scales=z_scale[:], in_=z_rows[:].rearrange("p c t -> p (c t)"))
 
-        h_bank = [psum.tile([P, S], F32, name=f"h_bank{t}") for t in range(PACK)]
-        for t in range(PACK):
+        sums = [(0, 0, W, psum.tile([P, W], F32, name="h_bank0")), (0, W, W, psum.tile([P, W], F32, name="h_half", tag="y_bank0"))]
+        sums += [(t, 0, S, psum.tile([P, S], F32, name=f"h_bank{t}")) for t in range(1, PACK)]
+        for t, c0, n, bank in sums:
             nc.tensor.matmul_mx(
-                out=h_bank[t][:],
+                out=bank[:],
                 lhsT=d2_word[:, P * t : P * (t + 1)].bitcast(FP8X4),
                 lhsT_scale=d_scale[:, S + P * t : S + P * (t + 1)],
-                rhs=xh_word[:].bitcast(FP8X4),
-                rhs_scale=placed[:, 2 * S : 3 * S],
+                rhs=xh_word[:, c0 : c0 + n].bitcast(FP8X4),
+                rhs_scale=placed[:, 2 * S + c0 : 2 * S + c0 + n],
                 start=True,
                 stop=False,
             )
-        for t in range(PACK):
+        for t, c0, n, bank in sums:
             nc.tensor.matmul_mx(
-                out=h_bank[t][:],
+                out=bank[:],
                 lhsT=d1_word[:, P * t : P * (t + 1)].bitcast(FP8X4),
                 lhsT_scale=d_scale[:, P * t : P * (t + 1)],
-                rhs=z_word[:].bitcast(FP8X4),
-                rhs_scale=z_scale[:],
+                rhs=z_word[:, c0 : c0 + n].bitcast(FP8X4),
+                rhs_scale=z_scale[:, c0 : c0 + n],
                 start=False,
                 stop=True,
             )
@@ -199,10 +217,11 @@ def tile_picked_cmixhhaarhpolar_none_p_kernel(
         result = [sb(f"result{t}", S, F32) for t in range(PACK)]
 
         def leave_bank(t):
-            if t == 1:
-                nc.vector.tensor_scalar_mul(h[t][:], h_bank[t][:], 0.0625)
+            if t == 0:
+                nc.scalar.activation(h[0][:, 0:W], sums[0][3][:], ACT.Copy, scale=0.0625)
+                nc.vector.tensor_scalar_mul(h[0][:, W:S], sums[1][3][:], 0.0625)
             else:
-                nc.scalar.activation(h[t][:], h_bank[t][:], ACT.Copy, scale=0.0625)
+                nc.scalar.activation(h[t][:], sums[t + 1][3][:], ACT.Copy, scale=0.0625)
 
         def pick(t):
             nc.scalar.activation(pair[t][:, 0:W], h[t][:].indirect(l_n4[:]), ACT.Copy, scale=-0.5)
@@ -223,14 +242,10 @@ def tile_picked_cmixhhaarhpolar_none_p_kernel(
             nc.vector.tensor_copy(result[t][:].indirect(l_n4[:]), root[:])
             nc.sync.dma_start(out_rows[t], result[t][:])
 
-        leave_bank(0)
-        leave_bank(1)
-        pick(0)
-        squares(0)
-        for t in range(1, PACK):
-            if t > 1:
-                leave_bank(t)
+        for t in range(PACK):
+            leave_bank(t)
             pick(t)
-            finish(t - 1)
             squares(t)
+            if t > 0:
+                finish(t - 1)
         finish(PACK - 1)

@@ -1,6 +1,7 @@
 from contextlib import ExitStack
 
 import concourse.mybir as mybir
+from concourse.masks import make_identity
 
 F32 = mybir.dt.float32
 BF16 = mybir.dt.bfloat16
@@ -47,6 +48,9 @@ def tile_picked_cmixhhaarhpolar_none_p_kernel(
         nc.vector.memset(placed[:].bitcast(I32), 0)
         nc.vector.memset(quarter[:], 0.25)
 
+        warm = sb("warm", 1, F32)
+        nc.scalar.activation(warm[:], quarter[:], ACT.Sqrt)
+
         x_tab = sb("x_tab", T, U32)
         w_raw = sb("w_raw", 2 * H, U8)
         gain = sb("gain", PACK, F32)
@@ -80,7 +84,7 @@ def tile_picked_cmixhhaarhpolar_none_p_kernel(
             w_raw[:].bitcast(U16).rearrange("p (m t) -> p t m", t=PACK),
         )
         nc.vector.tensor_copy(
-            w_scale[:].rearrange("p (t m) -> p m t", t=PACK), w_bytes[:].rearrange("p (m t) -> p m t", t=PACK)
+            w_scale[:].rearrange("p (t m) -> p t m", t=PACK), w_bytes[:].rearrange("p (m t) -> p t m", t=PACK)
         )
         d_tab = sb("d_tab", G, U32, tag="w_raw")
         nc.sync.dma_start(d_tab[:].bitcast(I32), d_words[0].rearrange("p n t -> p (n t)").bitcast(I32))
@@ -103,7 +107,7 @@ def tile_picked_cmixhhaarhpolar_none_p_kernel(
         for r in range(PACK):
             nc.sync.dma_start(placed[r:P:32, :].bitcast(I32), picked[8 * r : P : 32, :].bitcast(I32))
 
-        z_rows = keep.tile([P, S, PACK], BF16, name="z_rows", align_bytes=64)
+        z_rows = [keep.tile([P, W, PACK], BF16, name=f"z_rows{half}", align_bytes=64) for half in range(2)]
         dt = [sb(f"dt{t}", S, F32) for t in range(PACK)]
 
         pa = {}
@@ -142,7 +146,10 @@ def tile_picked_cmixhhaarhpolar_none_p_kernel(
             nc.vector.tensor_tensor(top[t][:], dt[t][:], other[t][:], ALU.max)
 
         def weigh(t):
-            nc.scalar.activation(z_rows[:, :, t], top[t][:], ACT.Copy, scale=gain[:, t : t + 1])
+            for half in range(2):
+                nc.scalar.activation(
+                    z_rows[half][:, :, t], top[t][:, W * half : W * (half + 1)], ACT.Copy, scale=gain[:, t : t + 1]
+                )
 
         def codewords(name, lst, tag):
             got = sb(f"{name}_got", H, U32, tag=tag)
@@ -162,22 +169,22 @@ def tile_picked_cmixhhaarhpolar_none_p_kernel(
         pair_sum(2)
         d_scale = sb("d_scale", 2 * S, U8, tag="y2")
         nc.vector.tensor_copy(
-            d_scale[:].rearrange("p (c t m) -> p c m t", c=2, t=PACK),
-            placed[:, 0 : 2 * S].rearrange("p (c m t) -> p c m t", c=2, t=PACK),
+            d_scale[:].rearrange("p (c t m) -> p c t m", c=2, t=PACK),
+            placed[:, 0 : 2 * S].rearrange("p (c m t) -> p c t m", c=2, t=PACK),
         )
         pair_difference(1)
         first_members(3)
         fetch(0)
-        pair_sum(3)
         pair_difference(2)
+        pair_sum(3)
         fetch(1)
         pair_difference(3)
         weigh(0)
-        d2_word = codewords("d2", l_k2, "top0")
+        xh_word = sb("xh_word", S, U32, tag="top0")
+        nc.vector.tensor_copy(xh_word[:], x_tab[:].indirect(l_hz[:]))
         fetch(2)
         weigh(1)
-        xh_word = sb("xh_word", S, U32, tag="top1")
-        nc.vector.tensor_copy(xh_word[:], x_tab[:].indirect(l_hz[:]))
+        d2_word = codewords("d2", l_k2, "top1")
         fetch(3)
         weigh(2)
         d1_word = codewords("d1", l_k1, "top2")
@@ -185,9 +192,15 @@ def tile_picked_cmixhhaarhpolar_none_p_kernel(
 
         z_word = sb("z_word", S, U32)
         z_scale = sb("z_scale", S, U8)
-        nc.vector.quantize_mx(out=z_word[:].bitcast(FP8X4), scales=z_scale[:], in_=z_rows[:].rearrange("p c t -> p (c t)"))
+        for half in range(2):
+            cols = slice(W * half, W * (half + 1))
+            nc.vector.quantize_mx(
+                out=z_word[:, cols].bitcast(FP8X4),
+                scales=z_scale[:, cols],
+                in_=z_rows[half][:].rearrange("p c t -> p (c t)"),
+            )
 
-        sums = [(0, 0, W, psum.tile([P, W], F32, name="h_bank0")), (0, W, W, psum.tile([P, W], F32, name="h_half", tag="y_bank0"))]
+        sums = [(0, 0, W, psum.tile([P, W], F32, name="h_bank0", tag="h_bank0")), (0, W, W, psum.tile([P, W], F32, name="h_half", tag="y_bank0"))]
         sums += [(t, 0, S, psum.tile([P, S], F32, name=f"h_bank{t}")) for t in range(1, PACK)]
         for t, c0, n, bank in sums:
             nc.tensor.matmul_mx(
@@ -213,7 +226,10 @@ def tile_picked_cmixhhaarhpolar_none_p_kernel(
         out_rows = out.rearrange("(p t) n -> t p n", t=PACK)
         h = [sb(f"h{t}", S, F32) for t in range(PACK)]
         pair = [sb(f"pair{t}", 2 * W, F32) for t in range(PACK)]
-        total = [sb(f"total{t}", W, F32) for t in range(PACK)]
+        total = {}
+        turned = {}
+        identity = sb("identity", P, F32)
+        make_identity(nc, identity[:])
         result = [sb(f"result{t}", S, F32) for t in range(PACK)]
 
         def leave_bank(t):
@@ -231,10 +247,27 @@ def tile_picked_cmixhhaarhpolar_none_p_kernel(
                 nc.scalar.activation(pair[t][:, W : 2 * W], h[t][:].indirect(l_n5[:]), ACT.Copy)
             nc.vector.tensor_tensor(result[t][:].indirect(l_n5[:]), pair[t][:, 0:W], pair[t][:, W : 2 * W], ALU.add)
 
+        def turn(t):
+            turned[t] = psum.tile([P, 2 * W], F32, name=f"turned{t}", tag=f"y_bank{1 + t % 2}")
+            for b in range(2 * W // P):
+                nc.tensor.transpose(turned[t][:, P * b : P * (b + 1)], pair[t][:, P * b : P * (b + 1)], identity[:])
+
         def squares(t):
             square = sb(f"square{t}", 2 * W, F32)
-            nc.scalar.activation(square[:], pair[t][:], ACT.Square)
-            nc.vector.scalar_tensor_tensor(total[t][:], square[:, 0:W], 4.0, square[:, W : 2 * W], ALU.mult, ALU.add)
+            nc.scalar.activation(square[:, 0:W], turned[t][:, 0:W], ACT.Square, scale=2.0)
+            nc.scalar.activation(square[:, W : 2 * W], turned[t][:, W : 2 * W], ACT.Square)
+            total[t] = psum.tile([P, W], F32, name=f"total{t}", tag=("y_bank3", "h_bank0")[t % 2])
+            for b in range(W // P):
+                for member in range(2):
+                    c0 = W * member + P * b
+                    nc.tensor.matmul(
+                        total[t][:, P * b : P * (b + 1)],
+                        lhsT=square[:, c0 : c0 + P],
+                        rhs=identity[:],
+                        is_transpose=True,
+                        start=(member == 0),
+                        stop=(member == 1),
+                    )
 
         def finish(t):
             root = sb(f"root{t}", W, F32)
@@ -242,10 +275,17 @@ def tile_picked_cmixhhaarhpolar_none_p_kernel(
             nc.vector.tensor_copy(result[t][:].indirect(l_n4[:]), root[:])
             nc.sync.dma_start(out_rows[t], result[t][:])
 
-        for t in range(PACK):
-            leave_bank(t)
+        leave_bank(0)
+        pick(0)
+        turn(0)
+        leave_bank(1)
+        for t in range(1, PACK):
             pick(t)
-            squares(t)
-            if t > 0:
-                finish(t - 1)
+            turn(t)
+            squares(t - 1)
+            if t + 1 < PACK:
+                leave_bank(t + 1)
+            else:
+                squares(t)
+            finish(t - 1)
         finish(PACK - 1)

from contextlib import ExitStack

import concourse.mybir as mybir
from concourse.masks import make_identity

F32 = mybir.dt.float32
BF16 = mybir.dt.bfloat16
I32 = mybir.dt.int32
U32 = mybir.dt.uint32
U16 = mybir.dt.uint16
U8 = mybir.dt.uint8
FP8X4 = mybir.dt.float8_e4m3fn_x4
FP4X4 = mybir.dt.float4_e2m1fn_x4
ACT = mybir.ActivationFunctionType
ALU = mybir.AluOpType

P = 128
PACK = 4
K, T, S, H, W, G = 512, 1024, 512, 512, 256, 2048
FLOPS = 3 * 2 * K * H * S


def tile_picked_cmixhhaarhpolar_none_p_kernel(
    tc, x_words, x_scales, w1_words, w1_scales, gs, d_words, d_scales, offs, n1, n2, n3, k1, k2, hz, n4, n5, out
):
    nc = tc.nc
    with ExitStack() as ctx:
        keep = ctx.enter_context(tc.tile_pool(name="keep", bufs=1))
        psum = ctx.enter_context(tc.psum_pool(name="psum", bufs=1))

        def sb(name, cols, dtype, tag=None):
            return keep.tile([P, cols], dtype, name=name, tag=tag or name, align_bytes=64)

        def load_list(name, src):
            tile = keep.tile([P, src.shape[1]], U16, name=name)
            nc.sync.dma_start(tile[:], src)
            return tile

        x_bytes = sb("x_bytes", T, U8)
        d_bytes = sb("d_bytes", G, U8)
        w_bytes = sb("w_bytes", H, U8)
        placed = sb("placed", 3 * S, U8)
        quarter = sb("quarter", 1, F32)
        nc.gpsimd.memset(x_bytes[:].bitcast(I32), 0)
        nc.gpsimd.memset(w_bytes[:].bitcast(I32), 0)
        nc.gpsimd.memset(d_bytes[:].bitcast(I32), 0)
        nc.gpsimd.dma_start(d_bytes[0:P:8, :].bitcast(I32), d_scales[0].bitcast(I32))
        nc.vector.memset(placed[:].bitcast(I32), 0)
        nc.vector.memset(quarter[:], 0.25)

        warm = sb("warm", 1, F32)
        nc.scalar.activation(warm[:], quarter[:], ACT.Sqrt)

        x_tab = sb("x_tab", T, U32)
        w_raw = sb("w_raw", 2 * H, U8)
        gain = sb("gain", PACK, F32)

        l_offs = load_list("l_offs", offs)
        nc.sync.dma_start(x_bytes[0:P:8, :].bitcast(I32), x_scales[0].bitcast(I32))
        for r in range(1, PACK):
            nc.sync.dma_start(x_bytes[r:P:32, :].bitcast(I32), x_scales[0][r:16:PACK, :].bitcast(I32))
        nc.sync.dma_start(x_tab[:].bitcast(I32), x_words[0].rearrange("p n t -> p (n t)").bitcast(I32))
        nc.sync.dma_start(w_raw[:].bitcast(I32), w1_words[0].bitcast(I32))
        l_hz = load_list("l_hz", hz)
        for r in range(PACK):
            nc.sync.dma_start(w_bytes[r:P:32, :].bitcast(I32), w1_scales[0][r:16:PACK, :].bitcast(I32))
        l_k1 = load_list("l_k1", k1)
        l_k2 = load_list("l_k2", k2)
        l_n1 = load_list("l_n1", n1)
        l_n2 = load_list("l_n2", n2)
        l_n3 = load_list("l_n3", n3)
        nc.sync.dma_start(gain[:], gs.rearrange("(p t) o -> p (t o)", t=PACK))
        l_n4 = load_list("l_n4", n4)
        l_n5 = load_list("l_n5", n5)

        xq_scale = sb("xq_scale", S, U8)
        xq_word = sb("xq_word", S, U32)
        nc.vector.tensor_copy(xq_scale[:], x_bytes[:].indirect(l_offs[:]))
        nc.vector.tensor_copy(xq_word[:], x_tab[:].indirect(l_offs[:]))
        w_word = sb("w_word", 2 * H, U8)
        w_scale = sb("w_scale", H, U8)
        nc.scalar.copy(
            w_word[:].bitcast(U16).rearrange("p (t m) -> p t m", t=PACK),
            w_raw[:].bitcast(U16).rearrange("p (m t) -> p t m", t=PACK),
        )
        nc.vector.tensor_copy(
            w_scale[:].rearrange("p (t m) -> p t m", t=PACK), w_bytes[:].rearrange("p (m t) -> p t m", t=PACK)
        )
        d_tab = sb("d_tab", G, U32, tag="w_raw")
        nc.sync.dma_start(d_tab[:].bitcast(I32), d_words[0].rearrange("p n t -> p (n t)").bitcast(I32))
        y_bank = [psum.tile([P, S], F32, name=f"y_bank{t}", tag=f"y_bank{t}") for t in range(PACK)]
        for t in range(PACK):
            nc.tensor.matmul_mx(
                out=y_bank[t][:],
                lhsT=w_word[:, 2 * P * t : 2 * P * (t + 1)].bitcast(FP4X4),
                lhsT_scale=w_scale[:, P * t : P * (t + 1)],
                rhs=xq_word[:].bitcast(FP8X4),
                rhs_scale=xq_scale[:],
                start=True,
                stop=True,
            )

        picked = sb("picked", 3 * S, U8)
        nc.vector.tensor_copy(picked[:, 2 * S : 3 * S], x_bytes[:].indirect(l_hz[:]))
        nc.vector.tensor_copy(picked[:, 0:S], d_bytes[:].indirect(l_k1[:]))
        nc.vector.tensor_copy(picked[:, S : 2 * S], d_bytes[:].indirect(l_k2[:]))
        for r in range(PACK):
            nc.sync.dma_start(placed[r:P:32, :].bitcast(I32), picked[8 * r : P : 32, :].bitcast(I32))

        z_rows = [keep.tile([P, W, PACK], BF16, name=f"z_rows{half}", align_bytes=64) for half in range(2)]
        dt = [sb(f"dt{t}", S, F32) for t in range(PACK)]

        pa = {}
        pb = {}

        y = {}

        def first_members(t):
            y[t] = sb(f"y{t}", S, F32)
            pa[t] = sb(f"pa{t}", W, F32)
            nc.scalar.activation(y[t][:], y_bank[t][:], ACT.Copy)
            nc.scalar.activation(pa[t][:], y[t][:].indirect(l_n1[:]), ACT.Copy)

        def pair_sum(t):
            pb[t] = sb(f"pb{t}", W, F32)
            nc.scalar.activation(pb[t][:], y[t][:].indirect(l_n2[:]), ACT.Copy)
            nc.vector.tensor_tensor(dt[t][:].indirect(l_n1[:]), pa[t][:], pb[t][:], ALU.add)

        def pair_difference(t):
            pb_neg = sb(f"pb_neg{t}", W, F32)
            nc.scalar.activation(pb_neg[:], pb[t][:], ACT.Copy, scale=-1.0)
            nc.vector.tensor_tensor(dt[t][:].indirect(l_n2[:]), pa[t][:], pb_neg[:], ALU.add)

        other = {}
        top = {}

        def fetch(t):
            other[t] = sb(f"other{t}", S, F32)
            for half in range(2):
                nc.scalar.activation(
                    other[t][:, W * half : W * (half + 1)],
                    dt[t][:].indirect(l_n3[:, 16 * half : 16 * (half + 1)]),
                    ACT.Copy,
                )
            top[t] = sb(f"top{t}", S, F32)
            nc.vector.tensor_tensor(top[t][:], dt[t][:], other[t][:], ALU.max)

        def weigh(t):
            for half in range(2):
                nc.scalar.activation(
                    z_rows[half][:, :, t], top[t][:, W * half : W * (half + 1)], ACT.Copy, scale=gain[:, t : t + 1]
                )

        def codewords(name, lst, tag):
            got = sb(f"{name}_got", H, U32, tag=tag)
            dealt = sb(f"{name}_word", H, U32)
            nc.vector.tensor_copy(got[:], d_tab[:].indirect(lst[:]))
            nc.vector.tensor_copy(
                dealt[:].rearrange("p (t m) -> p m t", t=PACK), got[:].rearrange("p (m t) -> p m t", t=PACK)
            )
            return dealt

        first_members(0)
        pair_sum(0)
        first_members(1)
        pair_sum(1)
        pair_difference(0)
        first_members(2)
        pair_sum(2)
        d_scale = sb("d_scale", 2 * S, U8, tag="y2")
        nc.vector.tensor_copy(
            d_scale[:].rearrange("p (c t m) -> p c t m", c=2, t=PACK),
            placed[:, 0 : 2 * S].rearrange("p (c m t) -> p c t m", c=2, t=PACK),
        )
        pair_difference(1)
        first_members(3)
        fetch(0)
        pair_difference(2)
        pair_sum(3)
        fetch(1)
        pair_difference(3)
        weigh(0)
        xh_word = sb("xh_word", S, U32, tag="top0")
        nc.vector.tensor_copy(xh_word[:], x_tab[:].indirect(l_hz[:]))
        fetch(2)
        weigh(1)
        d2_word = codewords("d2", l_k2, "top1")
        fetch(3)
        weigh(2)
        d1_word = codewords("d1", l_k1, "top2")
        weigh(3)

        z_word = sb("z_word", S, U32)
        z_scale = sb("z_scale", S, U8)
        for half in range(2):
            cols = slice(W * half, W * (half + 1))
            nc.vector.quantize_mx(
                out=z_word[:, cols].bitcast(FP8X4),
                scales=z_scale[:, cols],
                in_=z_rows[half][:].rearrange("p c t -> p (c t)"),
            )

        sums = [(0, 0, W, psum.tile([P, W], F32, name="h_bank0", tag="h_bank0")), (0, W, W, psum.tile([P, W], F32, name="h_half", tag="y_bank0"))]
        sums += [(t, 0, S, psum.tile([P, S], F32, name=f"h_bank{t}")) for t in range(1, PACK)]
        for t, c0, n, bank in sums:
            nc.tensor.matmul_mx(
                out=bank[:],
                lhsT=d2_word[:, P * t : P * (t + 1)].bitcast(FP8X4),
                lhsT_scale=d_scale[:, S + P * t : S + P * (t + 1)],
                rhs=xh_word[:, c0 : c0 + n].bitcast(FP8X4),
                rhs_scale=placed[:, 2 * S + c0 : 2 * S + c0 + n],
                start=True,
                stop=False,
            )
        for t, c0, n, bank in sums:
            nc.tensor.matmul_mx(
                out=bank[:],
                lhsT=d1_word[:, P * t : P * (t + 1)].bitcast(FP8X4),
                lhsT_scale=d_scale[:, P * t : P * (t + 1)],
                rhs=z_word[:, c0 : c0 + n].bitcast(FP8X4),
                rhs_scale=z_scale[:, c0 : c0 + n],
                start=False,
                stop=True,
            )

        out_rows = out.rearrange("(p t) n -> t p n", t=PACK)
        h = [sb(f"h{t}", S, F32) for t in range(PACK)]
        pair = [sb(f"pair{t}", 2 * W, F32) for t in range(PACK)]
        total = {}
        turned = {}
        identity = sb("identity", P, F32)
        make_identity(nc, identity[:])
        result = [sb(f"result{t}", S, F32) for t in range(PACK)]

        def leave_bank(t):
            if t == 0:
                nc.scalar.activation(h[0][:, 0:W], sums[0][3][:], ACT.Copy, scale=0.0625)
                nc.vector.tensor_scalar_mul(h[0][:, W:S], sums[1][3][:], 0.0625)
            else:
                nc.scalar.activation(h[t][:], sums[t + 1][3][:], ACT.Copy, scale=0.0625)

        def pick(t):
            nc.scalar.activation(pair[t][:, 0:W], h[t][:].indirect(l_n4[:]), ACT.Copy, scale=-0.5)
            if t == 0:
                nc.vector.tensor_copy(pair[t][:, W : 2 * W], h[t][:].indirect(l_n5[:]))
            else:
                nc.scalar.activation(pair[t][:, W : 2 * W], h[t][:].indirect(l_n5[:]), ACT.Copy)
            nc.vector.tensor_tensor(result[t][:].indirect(l_n5[:]), pair[t][:, 0:W], pair[t][:, W : 2 * W], ALU.add)

        def turn(t):
            turned[t] = psum.tile([P, 2 * W], F32, name=f"turned{t}", tag=f"y_bank{1 + t % 2}")
            for b in range(2 * W // P):
                nc.tensor.transpose(turned[t][:, P * b : P * (b + 1)], pair[t][:, P * b : P * (b + 1)], identity[:])

        def squares(t):
            square = sb(f"square{t}", 2 * W, F32)
            nc.scalar.activation(square[:, 0:W], turned[t][:, 0:W], ACT.Square, scale=2.0)
            nc.scalar.activation(square[:, W : 2 * W], turned[t][:, W : 2 * W], ACT.Square)
            total[t] = psum.tile([P, W], F32, name=f"total{t}", tag=("y_bank3", "h_bank0")[t % 2])
            for b in range(W // P):
                for member in range(2):
                    c0 = W * member + P * b
                    nc.tensor.matmul(
                        total[t][:, P * b : P * (b + 1)],
                        lhsT=square[:, c0 : c0 + P],
                        rhs=identity[:],
                        is_transpose=True,
                        start=(member == 0),
                        stop=(member == 1),
                    )

        def finish(t):
            root = sb(f"root{t}", W, F32)
            nc.scalar.activation(root[:], total[t][:], ACT.Sqrt, bias=quarter[:])
            nc.vector.tensor_copy(result[t][:].indirect(l_n4[:]), root[:])
            nc.sync.dma_start(out_rows[t], result[t][:])

        leave_bank(0)
        pick(0)
        turn(0)
        leave_bank(1)
        for t in range(1, PACK):
            pick(t)
            turn(t)
            squares(t - 1)
            if t + 1 < PACK:
                leave_bank(t + 1)
            else:
                squares(t)
            finish(t - 1)
        finish(PACK - 1)
